import numpy as np
import ml_dtypes


def mxq(x, axis, fmt="e4m3"):
    dtype, down = {"e4m3": (ml_dtypes.float8_e4m3fn, 7), "e5m2": (ml_dtypes.float8_e5m2, 14)}[fmt]
    v = np.moveaxis(np.asarray(x, np.float32).astype(ml_dtypes.bfloat16).astype(np.float64), axis, -1)
    blocks = v.reshape(v.shape[:-1] + (-1, 32))
    amax = np.abs(blocks).max(-1, keepdims=True)
    byte = np.maximum(np.where(amax > 0, np.frexp(amax)[1] - 1 + 127, 0) - down, 1)
    scale = np.exp2(byte - 127.0)
    codes = (blocks / scale).astype(np.float32).astype(dtype).astype(np.float64)
    return np.moveaxis((codes * scale).reshape(v.shape), -1, axis)


WIDE = False


def mx_kscale(k):
    if not WIDE:
        return np.ones(k)
    levels = np.array([10, -10, 5, -5, 0])
    if k % 512:
        return np.exp2(np.random.permutation(np.resize(levels, k // 32))).repeat(32)
    a = np.empty((k // 512, 16))
    for p in range(k // 512):
        a[p, :8] = np.random.permutation(np.resize(levels, 8))
        for g in range(8):
            far = levels[np.abs(levels - a[p, g]) >= 10]
            a[p, g + 8] = far[np.random.randint(len(far))]
    return np.exp2(a.ravel()).repeat(32)


def f64(x):
    return np.asarray(x).astype(np.float64)


def striped(idx):
    return np.tile(idx.reshape(-1, 16).T, (8, 1)).astype(np.uint16)


def unstriped(offs):
    return offs[:16].T.reshape(-1).astype(np.int64)


E2M1 = np.array([0.0, 0.5, 1.0, 1.5, 2.0, 3.0, 4.0, 6.0, -0.0, -0.5, -1.0, -1.5, -2.0, -3.0, -4.0, -6.0])


def pack_weight(w, fmt):
    k, n = w.shape
    w = f64(np.asarray(w, np.float32).astype(ml_dtypes.bfloat16)).reshape(k // 32, 32, n)
    amax = np.abs(w).max(1)
    if fmt == "e4m3":
        byte = np.frexp(amax)[1] - 1 + 127 - 7
    else:
        mant, ex = np.frexp(amax / 6.0)
        byte = np.where(mant > 0.5, ex, ex - 1) + 127
    byte = np.clip(np.where(amax > 0, byte, 1), 1, 254)
    scaled = (w * np.exp2(127.0 - byte)[:, None, :]).reshape(k, n).astype(np.float32)
    by_word = np.ascontiguousarray(scaled.reshape(k // 512, 128, 4, n).transpose(0, 1, 3, 2))
    if fmt == "e4m3":
        words = by_word.astype(ml_dtypes.float8_e4m3fn).view(np.uint8)
    else:
        c = by_word.astype(ml_dtypes.float4_e2m1fn).view(np.uint8) & 0xF
        words = (c[..., 0::2] | (c[..., 1::2] << 4)).reshape(k // 512, 128, 2 * n)
    return np.ascontiguousarray(words), np.ascontiguousarray(byte.astype(np.uint8).reshape(k // 512, 16, n))


def unpack_weight(words, scales, fmt):
    g, _, n = scales.shape
    words = np.ascontiguousarray(words).reshape(g, 128, n, -1)
    if fmt == "e4m3":
        vals = words.view(ml_dtypes.float8_e4m3fn).astype(np.float64)
    else:
        nib = np.empty((g, 128, n, 4), np.uint8)
        nib[..., 0::2] = words & 0xF
        nib[..., 1::2] = words >> 4
        vals = E2M1[nib]
    vals = vals * np.repeat(np.exp2(scales.astype(np.float64) - 127.0), 8, axis=1)[..., None]
    return vals.transpose(0, 1, 3, 2).reshape(g * 512, n)


def pack_table(v):
    words, scales = pack_weight(v, "e4m3")
    return np.concatenate([words.reshape(words.shape[0], -1), scales.reshape(scales.shape[0], -1)], axis=1)


def unpack_table(tab):
    g, t = tab.shape[0], tab.shape[1] // 528
    return unpack_weight(tab[:, :512 * t].reshape(g, 128, t, 4), tab[:, 512 * t:].reshape(g, 16, t), "e4m3")


K, R, M, T, S = 1536, 512, 1024, 4096, 1536


def setup_inputs():
    n = np.random.standard_normal
    s = mx_kscale(K)[:, None]
    u = mx_kscale(R)[:, None]
    p_w4 = pack_weight(n((K, M)) / np.sqrt(K) / s, "e2m1")
    return {
        "tab": pack_table(n((K, T)) * s),
        "w4_words": p_w4[0],
        "w4_scales": p_w4[1],
        "down": (n((K, R)) / np.sqrt(K) / s * u.T).astype(np.float32),
        "up": (0.5 * n((R, M)) / np.sqrt(R) / u).astype(np.float32),
        "prev": (n((1024, 1536))).astype(np.float32),
        "offs": striped(np.random.permutation(T)[:S]),
    }


def reference(tab, w4_words, w4_scales, down, up, prev, offs):
    tab_ = unpack_table(tab)[:, unstriped(offs)]
    w4_ = unpack_weight(w4_words, w4_scales, "e2m1")
    down_ = mxq(f64(down), 0, "e4m3")
    up_ = mxq(f64(up), 0, "e4m3")
    h_ = mxq(down_.T @ tab_, 0, "e4m3")
    y = w4_.T @ tab_ + up_.T @ h_
    return f64(prev) + y

@@ -1,0 +1,235 @@
+from contextlib import ExitStack
+
+import concourse.mybir as mybir
+
+K, R, M, T, S = 1536, 512, 1024, 4096, 1536
+
+FLOPS = 2 * S * (K * R + K * M + R * M)
+
+F32 = mybir.dt.float32
+BF16 = mybir.dt.bfloat16
+I32 = mybir.dt.int32
+U32 = mybir.dt.uint32
+U16 = mybir.dt.uint16
+U8 = mybir.dt.uint8
+FP8X4 = mybir.dt.float8_e4m3fn_x4
+FP4X4 = mybir.dt.float4_e2m1fn_x4
+ADD = mybir.AluOpType.add
+
+P = 128
+PASSES = K // 512
+NT = 512
+CHUNKS = S // NT
+RT = R // P
+MT = M // P
+
+
+def tile_list_tablora_res_kernel(
+    tc, tab, w4_words, w4_scales, down, up, prev, offs, out
+):
+    nc = tc.nc
+    with ExitStack() as ctx:
+        lists = ctx.enter_context(tc.tile_pool(name="lists", bufs=1))
+        keep = ctx.enter_context(tc.tile_pool(name="keep", bufs=1))
+        raws = ctx.enter_context(tc.tile_pool(name="raws", bufs=3))
+        grps = ctx.enter_context(tc.tile_pool(name="grps", bufs=3))
+        hbs = ctx.enter_context(tc.tile_pool(name="hbs", bufs=2))
+        psum = ctx.enter_context(tc.psum_pool(name="psum", bufs=8))
+
+        offsets = lists.tile([P, S // 16], U16, name="offsets")
+        nc.sync.dma_start(offsets[:], offs)
+
+        raw = [raws.tile([P, 4, R], F32, name="raw") for a in range(PASSES)]
+        win_w = [keep.tile([P, T], I32, name=f"win_w{a}", align_bytes=64) for a in range(PASSES)]
+        win_s = keep.tile([P, T // 4], I32, name="win_s", align_bytes=64)
+        w4w = keep.tile([P, PASSES, 2 * M], U8, name="w4w", align_bytes=64)
+        w4s = keep.tile([P, PASSES, M], U8, name="w4s", align_bytes=64)
+        up_raw = keep.tile([P, 4, M], F32, name="up_raw")
+        res = keep.tile([P, MT, S], F32, name="res")
+        moved = [keep.tile([P, S], U8, name=f"moved{a}", align_bytes=64) for a in range(1, PASSES)]
+
+        def load_pass(a):
+            nc.sync.dma_start(out=raw[a][:], in_=down[512 * a : 512 * (a + 1), :].rearrange("(p j) w -> p j w", j=4))
+            nc.sync.dma_start(
+                out=win_w[a][:], in_=tab[a, 0 : 512 * T].rearrange("(p b) -> p b", p=P).bitcast(I32)
+            )
+
+        load_pass(0)
+        nc.gpsimd.memset(win_s[:], 0)
+        rows = tab[:, 512 * T : 528 * T].rearrange("a (q t) -> a q t", q=16).bitcast(I32)
+        for q in range(4):
+            nc.gpsimd.dma_start(out=win_s[32 * q : 32 * q + 12, :], in_=rows[:, 4 * q : 4 * q + 4, :])
+        nc.gpsimd.memset(w4s[:].rearrange("p a n -> p (a n)").bitcast(I32), 0)
+        nc.gpsimd.memset(win_w[1][:, 0:1], 0)
+        nc.gpsimd.memset(raw[2][:, 0, 0:1], 0.0)
+        nc.gpsimd.memset(win_w[2][:, 0:1], 0)
+        nc.gpsimd.memset(w4w[:, 0, :].bitcast(I32)[:, 0:1], 0)
+        nc.gpsimd.memset(up_raw[:, 0, 0:1], 0.0)
+        for t in moved:
+            nc.vector.memset(t[:].bitcast(I32), 0)
+
+        load_pass(1)
+        load_pass(2)
+        nc.sync.dma_start(
+            out=w4w[:].bitcast(I32), in_=w4_words.bitcast(I32).rearrange("a p b -> p a b")
+        )
+        nc.sync.dma_start(out=up_raw[:], in_=up.rearrange("(p j) w -> p j w", j=4))
+        nc.vector.tensor_copy(res[:, :, 0:1], raw[2][:, 0, 0:MT].rearrange("p (m o) -> p m o", o=1))
+        for m in range(MT):
+            nc.sync.dma_start(out=res[:, m, :], in_=prev[P * m : P * (m + 1), :])
+        w4s_rows = w4_scales.bitcast(I32)
+        for q in range(4):
+            nc.gpsimd.dma_start(
+                out=w4s[32 * q : 32 * q + 4, :, :].bitcast(I32),
+                in_=w4s_rows[:, 4 * q : 4 * q + 4, :].rearrange("a r n -> r a n"),
+            )
+
+        dcodes, dscales = [], []
+
+        def quantize_down(a):
+            grp = grps.tile([P, 4 * R], BF16, name="grp", align_bytes=64)
+            nc.scalar.copy(
+                out=grp[:].rearrange("p (t m j) -> p m t j", t=4, j=4),
+                in_=raw[a][:].rearrange("p j (m t) -> p m t j", t=4),
+            )
+            c = keep.tile([P, R], U32, name=f"dcodes{a}", align_bytes=64)
+            s = keep.tile([P, R], U8, name=f"dscales{a}", align_bytes=64)
+            nc.vector.quantize_mx(out=c[:].bitcast(FP8X4), scales=s[:], in_=grp[:])
+            dcodes.append(c)
+            dscales.append(s)
+
+        gs = keep.tile([P, S], U8, name="gs", align_bytes=64)
+        gw = {}
+        OC = NT // 16
+
+        def gather_scales(n):
+            nc.vector.tensor_copy(
+                gs[:, NT * n : NT * (n + 1)],
+                win_s[:].bitcast(U8).indirect(offsets[:, OC * n : OC * (n + 1)]),
+            )
+
+        def gather_words(a, n):
+            t = keep.tile([P, NT], U32, name=f"gw{a}_{n}", align_bytes=64)
+            nc.vector.tensor_copy(
+                t[:], win_w[a][:].bitcast(U32).indirect(offsets[:, OC * n : OC * (n + 1)])
+            )
+            gw[a, n] = t
+
+        def h_pass(bank, a, n, t, start, stop):
+            nc.tensor.matmul_mx(
+                out=bank[:],
+                lhsT=dcodes[a][:, P * t : P * (t + 1)].bitcast(FP8X4),
+                lhsT_scale=dscales[a][:, P * t : P * (t + 1)],
+                rhs=gw[a, n][:].bitcast(FP8X4),
+                rhs_scale=gs[4 * a : P, NT * n : NT * (n + 1)],
+                start=start,
+                stop=stop,
+            )
+
+        def open_bank():
+            return psum.tile([P, NT], F32, name="bank")
+
+        quantize_down(0)
+        banks = {}
+        for n in (2, 0, 1):
+            gather_scales(n)
+            gather_words(0, n)
+        for n in (2, 0):
+            for t in range(RT):
+                banks[n, t] = open_bank()
+                h_pass(banks[n, t], 0, n, t, True, False)
+        for a in range(1, PASSES):
+            for q in range(4):
+                nc.gpsimd.dma_start(
+                    out=moved[a - 1][32 * q : 32 * q + 4, :].bitcast(I32),
+                    in_=gs[32 * q + 4 * a : 32 * q + 4 * a + 4, :].bitcast(I32),
+                )
+        quantize_down(1)
+        for n in (2, 0, 1):
+            gather_words(1, n)
+        part = []
+        for t in range(RT):
+            h_pass(banks[2, t], 1, 2, t, False, True)
+        for t in range(RT):
+            h_pass(banks[0, t], 1, 0, t, False, False)
+        for t in range(RT):
+            x = keep.tile([P, NT], F32, name=f"part{t}")
+            nc.scalar.copy(out=x[:], in_=banks[2, t][:])
+            part.append(x)
+        for t in range(RT):
+            banks[1, t] = open_bank()
+            for a in range(2):
+                h_pass(banks[1, t], a, 1, t, a == 0, False)
+        quantize_down(2)
+        for n in range(CHUNKS):
+            gather_words(2, n)
+        hb = []
+        for n in range(CHUNKS):
+            b = hbs.tile([P, RT, NT], BF16, name="hb")
+            hb.append(b)
+            for t in range(RT):
+                if n == 2:
+                    banks[n, t] = open_bank()
+                h_pass(banks[n, t], 2, n, t, n == 2, True)
+            for t in range(RT):
+                if n == 2:
+                    nc.vector.tensor_tensor(b[:, t, :], banks[n, t][:], part[t][:], ADD)
+                else:
+                    nc.scalar.copy(out=b[:, t, :], in_=banks[n, t][:])
+        hcodes, hscales = [], []
+        for n in range(CHUNKS):
+            grp = grps.tile([P, 4 * R], BF16, name="grp", align_bytes=64)
+            nc.vector.tensor_copy(
+                out=grp[:].rearrange("p (c t) -> p c t", t=4), in_=hb[n][:].rearrange("p t c -> p c t")
+            )
+            c = keep.tile([P, NT], U32, name=f"hcodes{n}", align_bytes=64)
+            s = keep.tile([P, NT], U8, name=f"hscales{n}", align_bytes=64)
+            nc.vector.quantize_mx(out=c[:].bitcast(FP8X4), scales=s[:], in_=grp[:])
+            hcodes.append(c)
+            hscales.append(s)
+
+        up_grp = keep.tile([P, M, 4], BF16, name="up_grp", align_bytes=64)
+        ucodes = keep.tile([P, M], U32, name="ucodes", align_bytes=64)
+        uscales = keep.tile([P, M], U8, name="uscales", align_bytes=64)
+        for i in range(2):
+            cols = slice(512 * i, 512 * (i + 1))
+            src = up_raw[:, :, cols].rearrange("p j c -> p c j")
+            if i == 0:
+                nc.scalar.copy(out=up_grp[:, cols, :], in_=src)
+            else:
+                nc.vector.tensor_copy(out=up_grp[:, cols, :], in_=src)
+            nc.vector.quantize_mx(
+                out=ucodes[:, cols].bitcast(FP8X4),
+                scales=uscales[:, cols],
+                in_=up_grp[:, cols, :].rearrange("p c j -> p (c j)"),
+            )
+
+        for m in range(MT):
+            for n in range(CHUNKS):
+                cols = slice(NT * n, NT * (n + 1))
+                y = open_bank()
+                for a in range(PASSES):
+                    plane = gs if a == 0 else moved[a - 1]
+                    nc.tensor.matmul_mx(
+                        out=y[:],
+                        lhsT=w4w[:, a, 256 * m : 256 * (m + 1)].bitcast(FP4X4),
+                        lhsT_scale=w4s[:, a, P * m : P * (m + 1)],
+                        rhs=gw[a, n][:].bitcast(FP8X4),
+                        rhs_scale=plane[:, cols],
+                        start=(a == 0),
+                        stop=False,
+                    )
+                nc.tensor.matmul_mx(
+                    out=y[:],
+                    lhsT=ucodes[:, P * m : P * (m + 1)].bitcast(FP8X4),
+                    lhsT_scale=uscales[:, P * m : P * (m + 1)],
+                    rhs=hcodes[n][:].bitcast(FP8X4),
+                    rhs_scale=hscales[n][:],
+                    start=False,
+                    stop=True,
+                )
+                nc.vector.tensor_tensor(res[:, m, cols], y[:], res[:, m, cols], ADD)
+                if m == MT - 1:
+                    nc.scalar.dma_start(out=out[P * m : P * (m + 1), cols], in_=res[:, m, cols])
+            if m < MT - 1:
+                nc.scalar.dma_start(out=out[P * m : P * (m + 1), :], in_=res[:, m, :])

@@ -55,16 +55,16 @@ def tile_list_tablora_res_kernel(
             )
 
         load_pass(0)
-        nc.gpsimd.memset(win_s[:], 0)
+        nc.vector.memset(win_s[:], 0)
         rows = tab[:, 512 * T : 528 * T].rearrange("a (q t) -> a q t", q=16).bitcast(I32)
         for q in range(4):
             nc.gpsimd.dma_start(out=win_s[32 * q : 32 * q + 12, :], in_=rows[:, 4 * q : 4 * q + 4, :])
         nc.gpsimd.memset(w4s[:].rearrange("p a n -> p (a n)").bitcast(I32), 0)
+        nc.gpsimd.memset(raw[1][:, 0, 0:1], 0.0)
         nc.gpsimd.memset(win_w[1][:, 0:1], 0)
         nc.gpsimd.memset(raw[2][:, 0, 0:1], 0.0)
         nc.gpsimd.memset(win_w[2][:, 0:1], 0)
         nc.gpsimd.memset(w4w[:, 0, :].bitcast(I32)[:, 0:1], 0)
-        nc.gpsimd.memset(up_raw[:, 0, 0:1], 0.0)
         for t in moved:
             nc.vector.memset(t[:].bitcast(I32), 0)
 
@@ -73,16 +73,14 @@ def tile_list_tablora_res_kernel(
         nc.sync.dma_start(
             out=w4w[:].bitcast(I32), in_=w4_words.bitcast(I32).rearrange("a p b -> p a b")
         )
-        nc.sync.dma_start(out=up_raw[:], in_=up.rearrange("(p j) w -> p j w", j=4))
-        nc.vector.tensor_copy(res[:, :, 0:1], raw[2][:, 0, 0:MT].rearrange("p (m o) -> p m o", o=1))
-        for m in range(MT):
-            nc.sync.dma_start(out=res[:, m, :], in_=prev[P * m : P * (m + 1), :])
         w4s_rows = w4_scales.bitcast(I32)
         for q in range(4):
             nc.gpsimd.dma_start(
                 out=w4s[32 * q : 32 * q + 4, :, :].bitcast(I32),
                 in_=w4s_rows[:, 4 * q : 4 * q + 4, :].rearrange("a r n -> r a n"),
             )
+        nc.vector.tensor_copy(up_raw[:, 0, 0:1], raw[2][:, 0, 0:1])
+        nc.sync.dma_start(out=up_raw[:], in_=up.rearrange("(p j) w -> p j w", j=4))
 
         dcodes, dscales = [], []
 
@@ -115,6 +113,11 @@ def tile_list_tablora_res_kernel(
             )
             gw[a, n] = t
 
+        def open_bank():
+            return psum.tile([P, NT], F32, name="bank")
+
+        LAST = CHUNKS - 1
+
         def h_pass(bank, a, n, t, start, stop):
             nc.tensor.matmul_mx(
                 out=bank[:],
@@ -126,18 +129,28 @@ def tile_list_tablora_res_kernel(
                 stop=stop,
             )
 
-        def open_bank():
-            return psum.tile([P, NT], F32, name="bank")
+        def h_last(bank, a, b, t, start, stop):
+            nc.tensor.matmul_mx(
+                out=bank[:, P * t : P * (t + 1)],
+                lhsT=dcodes[a][:, P * t : P * (t + 1)].bitcast(FP8X4),
+                lhsT_scale=dscales[a][:, P * t : P * (t + 1)],
+                rhs=gw[a, LAST][:, P * b : P * (b + 1)].bitcast(FP8X4),
+                rhs_scale=gs[4 * a : P, NT * LAST + P * b : NT * LAST + P * (b + 1)],
+                start=start,
+                stop=stop,
+            )
 
         quantize_down(0)
         banks = {}
-        for n in (2, 0, 1):
-            gather_scales(n)
-            gather_words(0, n)
-        for n in (2, 0):
-            for t in range(RT):
-                banks[n, t] = open_bank()
-                h_pass(banks[n, t], 0, n, t, True, False)
+        gather_scales(0)
+        gather_words(0, 0)
+        gather_scales(1)
+        gather_scales(2)
+        gather_words(0, 1)
+        gather_words(0, 2)
+        for t in range(RT):
+            banks[0, t] = open_bank()
+            h_pass(banks[0, t], 0, 0, t, True, False)
         for a in range(1, PASSES):
             for q in range(4):
                 nc.gpsimd.dma_start(
@@ -148,14 +161,16 @@ def tile_list_tablora_res_kernel(
         for n in (2, 0, 1):
             gather_words(1, n)
         part = []
-        for t in range(RT):
-            h_pass(banks[2, t], 1, 2, t, False, True)
+        for b in range(4):
+            bank = open_bank()
+            for t in range(RT):
+                for a in range(2):
+                    h_last(bank, a, b, t, a == 0, a == 1)
+            x = keep.tile([P, P, 4], F32, name=f"part{b}")
+            nc.scalar.copy(out=x[:], in_=bank[:].rearrange("p (t c) -> p c t", t=RT))
+            part.append(x)
         for t in range(RT):
             h_pass(banks[0, t], 1, 0, t, False, False)
-        for t in range(RT):
-            x = keep.tile([P, NT], F32, name=f"part{t}")
-            nc.scalar.copy(out=x[:], in_=banks[2, t][:])
-            part.append(x)
         for t in range(RT):
             banks[1, t] = open_bank()
             for a in range(2):
@@ -164,24 +179,34 @@ def tile_list_tablora_res_kernel(
         for n in range(CHUNKS):
             gather_words(2, n)
         hb = []
-        for n in range(CHUNKS):
-            b = hbs.tile([P, RT, NT], BF16, name="hb")
-            hb.append(b)
+        for n in range(LAST):
+            x = hbs.tile([P, RT, NT], BF16, name="hb")
+            hb.append(x)
             for t in range(RT):
-                if n == 2:
-                    banks[n, t] = open_bank()
-                h_pass(banks[n, t], 2, n, t, n == 2, True)
+                h_pass(banks[n, t], 2, n, t, False, True)
             for t in range(RT):
-                if n == 2:
-                    nc.vector.tensor_tensor(b[:, t, :], banks[n, t][:], part[t][:], ADD)
-                else:
-                    nc.scalar.copy(out=b[:, t, :], in_=banks[n, t][:])
+                nc.scalar.copy(out=x[:, t, :], in_=banks[n, t][:])
+        nc.vector.tensor_copy(res[:, :, 0:1], hb[0][:, 0, 0:MT].rearrange("p (m o) -> p m o", o=1))
+        for m in range(MT):
+            nc.sync.dma_start(out=res[:, m, :], in_=prev[P * m : P * (m + 1), :])
         hcodes, hscales = [], []
         for n in range(CHUNKS):
             grp = grps.tile([P, 4 * R], BF16, name="grp", align_bytes=64)
-            nc.vector.tensor_copy(
-                out=grp[:].rearrange("p (c t) -> p c t", t=4), in_=hb[n][:].rearrange("p t c -> p c t")
-            )
+            if n < LAST:
+                nc.vector.tensor_copy(
+                    out=grp[:].rearrange("p (c t) -> p c t", t=4), in_=hb[n][:].rearrange("p t c -> p c t")
+                )
+            else:
+                for b in range(4):
+                    bank = open_bank()
+                    for t in range(RT):
+                        h_last(bank, 2, b, t, True, True)
+                    nc.vector.tensor_tensor(
+                        grp[:, 512 * b : 512 * (b + 1)].rearrange("p (c t) -> p c t", t=4),
+                        bank[:].rearrange("p (t c) -> p c t", t=RT),
+                        part[b][:],
+                        ADD,
+                    )
             c = keep.tile([P, NT], U32, name=f"hcodes{n}", align_bytes=64)
             s = keep.tile([P, NT], U8, name=f"hscales{n}", align_bytes=64)
             nc.vector.quantize_mx(out=c[:].bitcast(FP8X4), scales=s[:], in_=grp[:])
@@ -191,13 +216,9 @@ def tile_list_tablora_res_kernel(
         up_grp = keep.tile([P, M, 4], BF16, name="up_grp", align_bytes=64)
         ucodes = keep.tile([P, M], U32, name="ucodes", align_bytes=64)
         uscales = keep.tile([P, M], U8, name="uscales", align_bytes=64)
-        for i in range(2):
-            cols = slice(512 * i, 512 * (i + 1))
-            src = up_raw[:, :, cols].rearrange("p j c -> p c j")
-            if i == 0:
-                nc.scalar.copy(out=up_grp[:, cols, :], in_=src)
-            else:
-                nc.vector.tensor_copy(out=up_grp[:, cols, :], in_=src)
+        for i in range(4):
+            cols = slice(256 * i, 256 * (i + 1))
+            nc.scalar.copy(out=up_grp[:, cols, :], in_=up_raw[:, :, cols].rearrange("p j c -> p c j"))
             nc.vector.quantize_mx(
                 out=ucodes[:, cols].bitcast(FP8X4),
                 scales=uscales[:, cols],

@@ -60,13 +60,13 @@ def tile_list_tablora_res_kernel(
         for q in range(4):
             nc.gpsimd.dma_start(out=win_s[32 * q : 32 * q + 12, :], in_=rows[:, 4 * q : 4 * q + 4, :])
         nc.gpsimd.memset(w4s[:].rearrange("p a n -> p (a n)").bitcast(I32), 0)
+        for t in moved:
+            nc.gpsimd.memset(t[:].bitcast(I32), 0)
         nc.gpsimd.memset(raw[1][:, 0, 0:1], 0.0)
         nc.gpsimd.memset(win_w[1][:, 0:1], 0)
         nc.gpsimd.memset(raw[2][:, 0, 0:1], 0.0)
         nc.gpsimd.memset(win_w[2][:, 0:1], 0)
         nc.gpsimd.memset(w4w[:, 0, :].bitcast(I32)[:, 0:1], 0)
-        for t in moved:
-            nc.vector.memset(t[:].bitcast(I32), 0)
 
         load_pass(1)
         load_pass(2)
@@ -79,17 +79,17 @@ def tile_list_tablora_res_kernel(
                 out=w4s[32 * q : 32 * q + 4, :, :].bitcast(I32),
                 in_=w4s_rows[:, 4 * q : 4 * q + 4, :].rearrange("a r n -> r a n"),
             )
-        nc.vector.tensor_copy(up_raw[:, 0, 0:1], raw[2][:, 0, 0:1])
-        nc.sync.dma_start(out=up_raw[:], in_=up.rearrange("(p j) w -> p j w", j=4))
 
         dcodes, dscales = [], []
 
         def quantize_down(a):
             grp = grps.tile([P, 4 * R], BF16, name="grp", align_bytes=64)
-            nc.scalar.copy(
-                out=grp[:].rearrange("p (t m j) -> p m t j", t=4, j=4),
-                in_=raw[a][:].rearrange("p j (m t) -> p m t j", t=4),
-            )
+            dst = grp[:].rearrange("p (t m j) -> p m t j", t=4, j=4)
+            src = raw[a][:].rearrange("p j (m t) -> p m t j", t=4)
+            m0 = P if a < PASSES - 1 else P // 2
+            nc.scalar.copy(out=dst[:, :m0, :, :], in_=src[:, :m0, :, :])
+            if m0 < P:
+                nc.vector.tensor_copy(out=dst[:, m0:, :, :], in_=src[:, m0:, :, :])
             c = keep.tile([P, R], U32, name=f"dcodes{a}", align_bytes=64)
             s = keep.tile([P, R], U8, name=f"dscales{a}", align_bytes=64)
             nc.vector.quantize_mx(out=c[:].bitcast(FP8X4), scales=s[:], in_=grp[:])
@@ -153,10 +153,12 @@ def tile_list_tablora_res_kernel(
             h_pass(banks[0, t], 0, 0, t, True, False)
         for a in range(1, PASSES):
             for q in range(4):
-                nc.gpsimd.dma_start(
+                (nc.sync if a == 1 else nc.gpsimd).dma_start(
                     out=moved[a - 1][32 * q : 32 * q + 4, :].bitcast(I32),
                     in_=gs[32 * q + 4 * a : 32 * q + 4 * a + 4, :].bitcast(I32),
                 )
+        nc.vector.tensor_copy(up_raw[:, 0, 0:1], raw[2][:, 0, 0:1])
+        nc.sync.dma_start(out=up_raw[:], in_=up.rearrange("(p j) w -> p j w", j=4))
         quantize_down(1)
         for n in (2, 0, 1):
             gather_words(1, n)
@@ -194,7 +196,8 @@ def tile_list_tablora_res_kernel(
             grp = grps.tile([P, 4 * R], BF16, name="grp", align_bytes=64)
             if n < LAST:
                 nc.vector.tensor_copy(
-                    out=grp[:].rearrange("p (c t) -> p c t", t=4), in_=hb[n][:].rearrange("p t c -> p c t")
+                    out=grp[:].rearrange("p (c i t) -> p c t i", i=4, t=4),
+                    in_=hb[n][:].rearrange("p t (c i) -> p c t i", i=4),
                 )
             else:
                 for b in range(4):
@@ -218,39 +221,49 @@ def tile_list_tablora_res_kernel(
         uscales = keep.tile([P, M], U8, name="uscales", align_bytes=64)
         for i in range(4):
             cols = slice(256 * i, 256 * (i + 1))
-            nc.scalar.copy(out=up_grp[:, cols, :], in_=up_raw[:, :, cols].rearrange("p j c -> p c j"))
+            nc.scalar.copy(
+                out=up_grp[:, cols, :].rearrange("p (c i) j -> p c j i", i=4),
+                in_=up_raw[:, :, cols].rearrange("p j (c i) -> p c j i", i=4),
+            )
             nc.vector.quantize_mx(
                 out=ucodes[:, cols].bitcast(FP8X4),
                 scales=uscales[:, cols],
                 in_=up_grp[:, cols, :].rearrange("p c j -> p (c j)"),
             )
 
-        for m in range(MT):
-            for n in range(CHUNKS):
-                cols = slice(NT * n, NT * (n + 1))
-                y = open_bank()
-                for a in range(PASSES):
-                    plane = gs if a == 0 else moved[a - 1]
-                    nc.tensor.matmul_mx(
-                        out=y[:],
-                        lhsT=w4w[:, a, 256 * m : 256 * (m + 1)].bitcast(FP4X4),
-                        lhsT_scale=w4s[:, a, P * m : P * (m + 1)],
-                        rhs=gw[a, n][:].bitcast(FP8X4),
-                        rhs_scale=plane[:, cols],
-                        start=(a == 0),
-                        stop=False,
-                    )
+        half = 2
+        order = [(m, n) for m in range(half) for n in range(LAST)]
+        order += [(m, LAST) for m in range(half)]
+        order += [(m, n) for m in range(half, MT) for n in range(CHUNKS)]
+        for m, n in order:
+            cols = slice(NT * n, NT * (n + 1))
+            y = open_bank()
+            for a in range(PASSES):
+                plane = gs if a == 0 else moved[a - 1]
                 nc.tensor.matmul_mx(
                     out=y[:],
-                    lhsT=ucodes[:, P * m : P * (m + 1)].bitcast(FP8X4),
-                    lhsT_scale=uscales[:, P * m : P * (m + 1)],
-                    rhs=hcodes[n][:].bitcast(FP8X4),
-                    rhs_scale=hscales[n][:],
-                    start=False,
-                    stop=True,
+                    lhsT=w4w[:, a, 256 * m : 256 * (m + 1)].bitcast(FP4X4),
+                    lhsT_scale=w4s[:, a, P * m : P * (m + 1)],
+                    rhs=gw[a, n][:].bitcast(FP8X4),
+                    rhs_scale=plane[:, cols],
+                    start=(a == 0),
+                    stop=False,
                 )
-                nc.vector.tensor_tensor(res[:, m, cols], y[:], res[:, m, cols], ADD)
+            nc.tensor.matmul_mx(
+                out=y[:],
+                lhsT=ucodes[:, P * m : P * (m + 1)].bitcast(FP8X4),
+                lhsT_scale=uscales[:, P * m : P * (m + 1)],
+                rhs=hcodes[n][:].bitcast(FP8X4),
+                rhs_scale=hscales[n][:],
+                start=False,
+                stop=True,
+            )
+            halves = 2 if m == MT - 1 and n == LAST else 1
+            w = NT // halves
+            for i in range(halves):
+                part_cols = slice(NT * n + w * i, NT * n + w * (i + 1))
+                nc.vector.tensor_tensor(res[:, m, part_cols], y[:, w * i : w * (i + 1)], res[:, m, part_cols], ADD)
                 if m == MT - 1:
-                    nc.scalar.dma_start(out=out[P * m : P * (m + 1), cols], in_=res[:, m, cols])
-            if m < MT - 1:
+                    nc.scalar.dma_start(out=out[P * m : P * (m + 1), part_cols], in_=res[:, m, part_cols])
+            if m < MT - 1 and n == LAST:
                 nc.scalar.dma_start(out=out[P * m : P * (m + 1), :], in_=res[:, m, :])

from contextlib import ExitStack

import concourse.mybir as mybir

K, R, M, T, S = 1536, 512, 1024, 4096, 1536

FLOPS = 2 * S * (K * R + K * M + R * M)

F32 = mybir.dt.float32
BF16 = mybir.dt.bfloat16
I32 = mybir.dt.int32
U32 = mybir.dt.uint32
U16 = mybir.dt.uint16
U8 = mybir.dt.uint8
FP8X4 = mybir.dt.float8_e4m3fn_x4
FP4X4 = mybir.dt.float4_e2m1fn_x4
ADD = mybir.AluOpType.add

P = 128
PASSES = K // 512
NT = 512
CHUNKS = S // NT
RT = R // P
MT = M // P


def tile_list_tablora_res_kernel(
    tc, tab, w4_words, w4_scales, down, up, prev, offs, out
):
    nc = tc.nc
    with ExitStack() as ctx:
        lists = ctx.enter_context(tc.tile_pool(name="lists", bufs=1))
        keep = ctx.enter_context(tc.tile_pool(name="keep", bufs=1))
        raws = ctx.enter_context(tc.tile_pool(name="raws", bufs=3))
        grps = ctx.enter_context(tc.tile_pool(name="grps", bufs=3))
        hbs = ctx.enter_context(tc.tile_pool(name="hbs", bufs=2))
        psum = ctx.enter_context(tc.psum_pool(name="psum", bufs=8))

        offsets = lists.tile([P, S // 16], U16, name="offsets")
        nc.sync.dma_start(offsets[:], offs)

        raw = [raws.tile([P, 4, R], F32, name="raw") for a in range(PASSES)]
        win_w = [keep.tile([P, T], I32, name=f"win_w{a}", align_bytes=64) for a in range(PASSES)]
        win_s = keep.tile([P, T // 4], I32, name="win_s", align_bytes=64)
        w4w = keep.tile([P, PASSES, 2 * M], U8, name="w4w", align_bytes=64)
        w4s = keep.tile([P, PASSES, M], U8, name="w4s", align_bytes=64)
        up_raw = keep.tile([P, 4, M], F32, name="up_raw")
        res = keep.tile([P, MT, S], F32, name="res")
        moved = [keep.tile([P, S], U8, name=f"moved{a}", align_bytes=64) for a in range(1, PASSES)]

        def load_pass(a):
            nc.sync.dma_start(out=raw[a][:], in_=down[512 * a : 512 * (a + 1), :].rearrange("(p j) w -> p j w", j=4))
            nc.sync.dma_start(
                out=win_w[a][:], in_=tab[a, 0 : 512 * T].rearrange("(p b) -> p b", p=P).bitcast(I32)
            )

        load_pass(0)
        nc.vector.memset(win_s[:], 0)
        rows = tab[:, 512 * T : 528 * T].rearrange("a (q t) -> a q t", q=16).bitcast(I32)
        for q in range(4):
            nc.gpsimd.dma_start(out=win_s[32 * q : 32 * q + 12, :], in_=rows[:, 4 * q : 4 * q + 4, :])
        nc.gpsimd.memset(w4s[:].rearrange("p a n -> p (a n)").bitcast(I32), 0)
        for t in moved:
            nc.gpsimd.memset(t[:].bitcast(I32), 0)
        nc.gpsimd.memset(raw[1][:, 0, 0:1], 0.0)
        nc.gpsimd.memset(win_w[1][:, 0:1], 0)
        nc.gpsimd.memset(raw[2][:, 0, 0:1], 0.0)
        nc.gpsimd.memset(win_w[2][:, 0:1], 0)
        nc.gpsimd.memset(w4w[:, 0, :].bitcast(I32)[:, 0:1], 0)

        load_pass(1)
        load_pass(2)
        nc.sync.dma_start(
            out=w4w[:].bitcast(I32), in_=w4_words.bitcast(I32).rearrange("a p b -> p a b")
        )
        w4s_rows = w4_scales.bitcast(I32)
        for q in range(4):
            nc.gpsimd.dma_start(
                out=w4s[32 * q : 32 * q + 4, :, :].bitcast(I32),
                in_=w4s_rows[:, 4 * q : 4 * q + 4, :].rearrange("a r n -> r a n"),
            )

        dcodes, dscales = [], []

        def quantize_down(a):
            grp = grps.tile([P, 4 * R], BF16, name="grp", align_bytes=64)
            dst = grp[:].rearrange("p (t m j) -> p m t j", t=4, j=4)
            src = raw[a][:].rearrange("p j (m t) -> p m t j", t=4)
            m0 = P if a < PASSES - 1 else P // 2
            nc.scalar.copy(out=dst[:, :m0, :, :], in_=src[:, :m0, :, :])
            if m0 < P:
                nc.vector.tensor_copy(out=dst[:, m0:, :, :], in_=src[:, m0:, :, :])
            c = keep.tile([P, R], U32, name=f"dcodes{a}", align_bytes=64)
            s = keep.tile([P, R], U8, name=f"dscales{a}", align_bytes=64)
            nc.vector.quantize_mx(out=c[:].bitcast(FP8X4), scales=s[:], in_=grp[:])
            dcodes.append(c)
            dscales.append(s)

        gs = keep.tile([P, S], U8, name="gs", align_bytes=64)
        gw = {}
        OC = NT // 16

        def gather_scales(n):
            nc.vector.tensor_copy(
                gs[:, NT * n : NT * (n + 1)],
                win_s[:].bitcast(U8).indirect(offsets[:, OC * n : OC * (n + 1)]),
            )

        def gather_words(a, n):
            t = keep.tile([P, NT], U32, name=f"gw{a}_{n}", align_bytes=64)
            nc.vector.tensor_copy(
                t[:], win_w[a][:].bitcast(U32).indirect(offsets[:, OC * n : OC * (n + 1)])
            )
            gw[a, n] = t

        def open_bank():
            return psum.tile([P, NT], F32, name="bank")

        LAST = CHUNKS - 1

        def h_pass(bank, a, n, t, start, stop):
            nc.tensor.matmul_mx(
                out=bank[:],
                lhsT=dcodes[a][:, P * t : P * (t + 1)].bitcast(FP8X4),
                lhsT_scale=dscales[a][:, P * t : P * (t + 1)],
                rhs=gw[a, n][:].bitcast(FP8X4),
                rhs_scale=gs[4 * a : P, NT * n : NT * (n + 1)],
                start=start,
                stop=stop,
            )

        def h_last(bank, a, b, t, start, stop):
            nc.tensor.matmul_mx(
                out=bank[:, P * t : P * (t + 1)],
                lhsT=dcodes[a][:, P * t : P * (t + 1)].bitcast(FP8X4),
                lhsT_scale=dscales[a][:, P * t : P * (t + 1)],
                rhs=gw[a, LAST][:, P * b : P * (b + 1)].bitcast(FP8X4),
                rhs_scale=gs[4 * a : P, NT * LAST + P * b : NT * LAST + P * (b + 1)],
                start=start,
                stop=stop,
            )

        quantize_down(0)
        banks = {}
        gather_scales(0)
        gather_words(0, 0)
        gather_scales(1)
        gather_scales(2)
        gather_words(0, 1)
        gather_words(0, 2)
        for t in range(RT):
            banks[0, t] = open_bank()
            h_pass(banks[0, t], 0, 0, t, True, False)
        for a in range(1, PASSES):
            for q in range(4):
                (nc.sync if a == 1 else nc.gpsimd).dma_start(
                    out=moved[a - 1][32 * q : 32 * q + 4, :].bitcast(I32),
                    in_=gs[32 * q + 4 * a : 32 * q + 4 * a + 4, :].bitcast(I32),
                )
        nc.vector.tensor_copy(up_raw[:, 0, 0:1], raw[2][:, 0, 0:1])
        nc.sync.dma_start(out=up_raw[:], in_=up.rearrange("(p j) w -> p j w", j=4))
        quantize_down(1)
        for n in (2, 0, 1):
            gather_words(1, n)
        part = []
        for b in range(4):
            bank = open_bank()
            for t in range(RT):
                for a in range(2):
                    h_last(bank, a, b, t, a == 0, a == 1)
            x = keep.tile([P, P, 4], F32, name=f"part{b}")
            nc.scalar.copy(out=x[:], in_=bank[:].rearrange("p (t c) -> p c t", t=RT))
            part.append(x)
        for t in range(RT):
            h_pass(banks[0, t], 1, 0, t, False, False)
        for t in range(RT):
            banks[1, t] = open_bank()
            for a in range(2):
                h_pass(banks[1, t], a, 1, t, a == 0, False)
        quantize_down(2)
        for n in range(CHUNKS):
            gather_words(2, n)
        hb = []
        for n in range(LAST):
            x = hbs.tile([P, RT, NT], BF16, name="hb")
            hb.append(x)
            for t in range(RT):
                h_pass(banks[n, t], 2, n, t, False, True)
            for t in range(RT):
                nc.scalar.copy(out=x[:, t, :], in_=banks[n, t][:])
        nc.vector.tensor_copy(res[:, :, 0:1], hb[0][:, 0, 0:MT].rearrange("p (m o) -> p m o", o=1))
        for m in range(MT):
            nc.sync.dma_start(out=res[:, m, :], in_=prev[P * m : P * (m + 1), :])
        hcodes, hscales = [], []
        for n in range(CHUNKS):
            grp = grps.tile([P, 4 * R], BF16, name="grp", align_bytes=64)
            if n < LAST:
                nc.vector.tensor_copy(
                    out=grp[:].rearrange("p (c i t) -> p c t i", i=4, t=4),
                    in_=hb[n][:].rearrange("p t (c i) -> p c t i", i=4),
                )
            else:
                for b in range(4):
                    bank = open_bank()
                    for t in range(RT):
                        h_last(bank, 2, b, t, True, True)
                    nc.vector.tensor_tensor(
                        grp[:, 512 * b : 512 * (b + 1)].rearrange("p (c t) -> p c t", t=4),
                        bank[:].rearrange("p (t c) -> p c t", t=RT),
                        part[b][:],
                        ADD,
                    )
            c = keep.tile([P, NT], U32, name=f"hcodes{n}", align_bytes=64)
            s = keep.tile([P, NT], U8, name=f"hscales{n}", align_bytes=64)
            nc.vector.quantize_mx(out=c[:].bitcast(FP8X4), scales=s[:], in_=grp[:])
            hcodes.append(c)
            hscales.append(s)

        up_grp = keep.tile([P, M, 4], BF16, name="up_grp", align_bytes=64)
        ucodes = keep.tile([P, M], U32, name="ucodes", align_bytes=64)
        uscales = keep.tile([P, M], U8, name="uscales", align_bytes=64)
        for i in range(4):
            cols = slice(256 * i, 256 * (i + 1))
            nc.scalar.copy(
                out=up_grp[:, cols, :].rearrange("p (c i) j -> p c j i", i=4),
                in_=up_raw[:, :, cols].rearrange("p j (c i) -> p c j i", i=4),
            )
            nc.vector.quantize_mx(
                out=ucodes[:, cols].bitcast(FP8X4),
                scales=uscales[:, cols],
                in_=up_grp[:, cols, :].rearrange("p c j -> p (c j)"),
            )

        half = 2
        order = [(m, n) for m in range(half) for n in range(LAST)]
        order += [(m, LAST) for m in range(half)]
        order += [(m, n) for m in range(half, MT) for n in range(CHUNKS)]
        for m, n in order:
            cols = slice(NT * n, NT * (n + 1))
            y = open_bank()
            for a in range(PASSES):
                plane = gs if a == 0 else moved[a - 1]
                nc.tensor.matmul_mx(
                    out=y[:],
                    lhsT=w4w[:, a, 256 * m : 256 * (m + 1)].bitcast(FP4X4),
                    lhsT_scale=w4s[:, a, P * m : P * (m + 1)],
                    rhs=gw[a, n][:].bitcast(FP8X4),
                    rhs_scale=plane[:, cols],
                    start=(a == 0),
                    stop=False,
                )
            nc.tensor.matmul_mx(
                out=y[:],
                lhsT=ucodes[:, P * m : P * (m + 1)].bitcast(FP8X4),
                lhsT_scale=uscales[:, P * m : P * (m + 1)],
                rhs=hcodes[n][:].bitcast(FP8X4),
                rhs_scale=hscales[n][:],
                start=False,
                stop=True,
            )
            halves = 2 if m == MT - 1 and n == LAST else 1
            w = NT // halves
            for i in range(halves):
                part_cols = slice(NT * n + w * i, NT * n + w * (i + 1))
                nc.vector.tensor_tensor(res[:, m, part_cols], y[:, w * i : w * (i + 1)], res[:, m, part_cols], ADD)
                if m == MT - 1:
                    nc.scalar.dma_start(out=out[P * m : P * (m + 1), part_cols], in_=res[:, m, part_cols])
            if m < MT - 1 and n == LAST:
                nc.scalar.dma_start(out=out[P * m : P * (m + 1), :], in_=res[:, m, :])
